import numpy as np
import ml_dtypes


def mxq(x, axis, fmt="e4m3"):
    dtype, down = {"e4m3": (ml_dtypes.float8_e4m3fn, 7), "e5m2": (ml_dtypes.float8_e5m2, 14)}[fmt]
    v = np.moveaxis(np.asarray(x, np.float32).astype(ml_dtypes.bfloat16).astype(np.float64), axis, -1)
    blocks = v.reshape(v.shape[:-1] + (-1, 32))
    amax = np.abs(blocks).max(-1, keepdims=True)
    byte = np.maximum(np.where(amax > 0, np.frexp(amax)[1] - 1 + 127, 0) - down, 1)
    scale = np.exp2(byte - 127.0)
    codes = (blocks / scale).astype(np.float32).astype(dtype).astype(np.float64)
    return np.moveaxis((codes * scale).reshape(v.shape), -1, axis)


WIDE = False


def mx_kscale(k, group=512):
    if not WIDE:
        return np.ones(k)
    levels = np.array([18, -18])
    if group != 512:
        return np.exp2(np.random.permutation(np.resize(levels, k // group))).repeat(group)
    if k % 512:
        return np.exp2(np.random.permutation(np.resize(levels, k // 32))).repeat(32)
    a = np.empty((k // 512, 16))
    for p in range(k // 512):
        a[p, :8] = np.random.permutation(np.resize(levels, 8))
        for g in range(8):
            far = levels[np.abs(levels - a[p, g]) >= 10]
            a[p, g + 8] = far[np.random.randint(len(far))]
    return np.exp2(a.ravel()).repeat(32)


def f64(x):
    return np.asarray(x).astype(np.float64)


G, D, M, O, N = 4, 128, 128, 128, 512


def sgn(shape):
    return np.random.uniform(0.5, 2.0, shape) * np.where(np.random.standard_normal(shape) < 0, -1.0, 1.0)


def setup_inputs():
    n = np.random.standard_normal
    s_d = mx_kscale(D, 0)
    s_m = mx_kscale(M, 0)
    return {
        "x": (n((G, D, N)) * s_d[:, None]).astype(np.float32),
        "w1": (n((G, D, M)) / np.sqrt(D) / s_d[:, None]).astype(np.float32),
        "w2": (n((G, D, M)) / np.sqrt(D) / s_d[:, None]).astype(np.float32),
        "w3": (n((G, D, M)) / np.sqrt(D) / s_d[:, None]).astype(np.float32),
        "re": (np.random.uniform(0.3, 1.5, (G, M, 1))).astype(np.float32),
        "hs": (sgn((G, M, 1)) * s_m[:, None]).astype(np.float32),
        "wo2": (n((G, M, O)) / np.sqrt(M) / s_m[:, None]).astype(np.float32),
        "res": (0.5 * n((G, O, N))).astype(np.float32),
    }


def reference(x, w1, w2, w3, re, hs, wo2, res):
    w1q = mxq(f64(w1), 1, "e4m3")
    xq = mxq(f64(x), 1, "e4m3")
    z1 = w1q.transpose(0, 2, 1) @ xq
    w2q = mxq(f64(w2), 1, "e4m3")
    z2 = w2q.transpose(0, 2, 1) @ xq
    w3q = mxq(f64(w3), 1, "e4m3")
    z3 = w3q.transpose(0, 2, 1) @ xq
    e1 = np.exp(z1)
    e2 = np.exp(z2)
    h = e1 / (e1 + e2 + f64(re)) * z3
    hh = h * f64(hs)
    wo2q = mxq(f64(wo2), 1, "e4m3")
    hhq = mxq(hh, 1, "e4m3")
    y0 = wo2q.transpose(0, 2, 1) @ hhq
    y = y0 + f64(res)
    return y

@@ -1,0 +1,209 @@
+from contextlib import ExitStack
+
+import concourse.mybir as mybir
+
+G, D, M, O, N = 4, 128, 128, 128, 512
+FLOPS = 2 * G * N * (3 * D * M + M * O)
+
+F32 = mybir.dt.float32
+BF16 = mybir.dt.bfloat16
+U32 = mybir.dt.uint32
+U8 = mybir.dt.uint8
+FP8X4 = mybir.dt.float8_e4m3fn_x4
+ACT = mybir.ActivationFunctionType
+ALU = mybir.AluOpType
+
+P = 128
+PACK = 4
+ROWS = 32
+HALF = N // 2
+MM_N = 128
+V_COLS = 160
+
+
+def tile_rows_ftwoshare_kernel(tc, x, w1, w2, w3, re, hs, wo2, res, out):
+    nc = tc.nc
+    with ExitStack() as ctx:
+        sb = ctx.enter_context(tc.tile_pool(name="sb", bufs=1))
+        ps = ctx.enter_context(tc.psum_pool(name="ps", bufs=1))
+        ctx.enter_context(tc.manual_schedule())
+
+        def tile(name, shape, dtype):
+            return sb.tile(shape, dtype, name=name, align_bytes=64)
+
+        def load_packed(name, src, cols):
+            raw = tile(name, [P, PACK, cols.stop - cols.start], F32)
+            nc.sync.dma_start(out=raw[:], in_=src.rearrange("g (p j) c -> (g p) j c", j=PACK)[:, :, cols])
+            return raw
+
+        def views(dst, raw, lo, hi):
+            return (
+                dst[:, lo:hi, :].rearrange("p (c i) j -> p c j i", i=4),
+                raw[:, :, lo:hi].rearrange("p j (c i) -> p c j i", i=4),
+            )
+
+        def interleave_v(dst, raw, lo, hi):
+            o, i = views(dst, raw, lo, hi)
+            nc.vector.tensor_copy(out=o, in_=i)
+
+        def interleave_s(dst, raw, lo, hi):
+            o, i = views(dst, raw, lo, hi)
+            nc.scalar.copy(out=o, in_=i)
+
+        def quantize(name, grouped, width):
+            codes = tile(name + "_codes", [P, width], U32)
+            scales = tile(name + "_scales", [P, width], U8)
+            nc.vector.quantize_mx(
+                out=codes[:].bitcast(FP8X4),
+                scales=scales[:],
+                in_=grouped[:].rearrange("p c j -> p (c j)"),
+            )
+            return codes, scales
+
+        def product(bank, at, weights, moving, g):
+            rows = slice(ROWS * g, ROWS * (g + 1))
+            for c in range(0, HALF, MM_N):
+                nc.tensor.matmul_mx(
+                    out=bank[:, at + c : at + c + MM_N],
+                    lhsT=weights[0][rows, :].bitcast(FP8X4),
+                    lhsT_scale=weights[1][rows, :],
+                    rhs=moving[0][rows, c : c + MM_N].bitcast(FP8X4),
+                    rhs_scale=moving[1][rows, c : c + MM_N],
+                    start=True,
+                    stop=True,
+                )
+
+        banks = [[ps.tile([P, N], F32, name="bank%d_%d" % (h, g)) for g in range(G)] for h in range(2)]
+
+        rows_in = tile("rows_in", [P, 2 * G * ROWS], F32)
+        nc.vector.memset(rows_in[:], 0.0)
+        for k, src in enumerate((re, hs)):
+            nc.scalar.dma_start(
+                out=rows_in[0:P:ROWS, k * P : (k + 1) * P].rearrange("q (g b) -> q g b", g=G),
+                in_=src.rearrange("g (q b) o -> q g (b o)", b=ROWS),
+            )
+
+        all_m = slice(0, M)
+        halves = [slice(0, HALF), slice(HALF, N)]
+        w2_raw = load_packed("w2_raw", w2, all_m)
+        xa_raw = load_packed("xa_raw", x, halves[0])
+        w1_raw = load_packed("w1_raw", w1, all_m)
+        xb_raw = load_packed("xb_raw", x, halves[1])
+        w3_raw = load_packed("w3_raw", w3, all_m)
+        wo_raw = load_packed("wo_raw", wo2, all_m)
+        res_sb = tile("res_sb", [P, G, N], F32)
+        nc.sync.dma_start(out=res_sb[:], in_=res.rearrange("g o n -> o g n"))
+
+        w2_bf = tile("w2_bf", [P, M, PACK], BF16)
+        interleave_v(w2_bf, w2_raw, 0, M)
+        columns = tile("columns", [P, 2 * G * ROWS], F32)
+        nc.vector.transpose(out=columns[:], in_=rows_in[:])
+        w2q = quantize("w2", w2_bf, M)
+
+        xa_bf = tile("xa_bf", [P, HALF, PACK], BF16)
+        interleave_v(xa_bf, xa_raw, 0, V_COLS)
+        interleave_s(xa_bf, xa_raw, V_COLS, HALF)
+        xaq = quantize("xa", xa_bf, HALF)
+        w1_bf = tile("w1_bf", [P, M, PACK], BF16)
+        interleave_s(w1_bf, w1_raw, 0, M)
+        w1q = quantize("w1", w1_bf, M)
+        xb_bf = tile("xb_bf", [P, HALF, PACK], BF16)
+        interleave_v(xb_bf, xb_raw, 0, HALF)
+        xbq = quantize("xb", xb_bf, HALF)
+        xq = [xaq, xbq]
+
+        e2 = [[tile("e2_%d_%d" % (h, g), [P, HALF], F32) for g in range(G)] for h in range(2)]
+        inv_e1 = [[tile("inv_e1_%d_%d" % (h, g), [P, HALF], F32) for g in range(G)] for h in range(2)]
+        odds = [tile("odds_%d" % h, [P, G * HALF], F32) for h in range(2)]
+        square = [tile("square_%d" % h, [P, G * HALF], F32) for h in range(2)]
+
+        def exp_z2(h, g):
+            nc.scalar.activation(out=e2[h][g][:], in_=banks[h][g][:, 0:HALF], func=ACT.Exp)
+
+        def exp_minus_z1(h, g):
+            nc.scalar.activation(out=inv_e1[h][g][:], in_=banks[h][g][:, HALF:N], func=ACT.Exp, scale=-1.0)
+
+        def make_odds(h, g):
+            nc.vector.scalar_tensor_tensor(
+                out=odds[h][:, g * HALF : (g + 1) * HALF],
+                in0=e2[h][g][:],
+                scalar=columns[:, ROWS * g : ROWS * g + 1],
+                in1=inv_e1[h][g][:],
+                op0=ALU.add,
+                op1=ALU.mult,
+            )
+
+        def make_square(h, lo, hi):
+            cols = slice(lo * HALF, hi * HALF)
+            nc.vector.scalar_tensor_tensor(
+                out=square[h][:, cols],
+                in0=odds[h][:, cols],
+                scalar=2.0,
+                in1=odds[h][:, cols],
+                op0=ALU.add,
+                op1=ALU.mult,
+            )
+
+        for g in range(G):
+            product(banks[0][g], 0, w2q, xq[0], g)
+            exp_z2(0, g)
+        for g in range(G):
+            product(banks[0][g], HALF, w1q, xq[0], g)
+            exp_minus_z1(0, g)
+            make_odds(0, g)
+        w3_bf = tile("w3_bf", [P, M, PACK], BF16)
+        interleave_v(w3_bf, w3_raw, 0, M)
+        make_square(0, 0, G)
+        w3q = quantize("w3", w3_bf, M)
+        for g in range(G):
+            product(banks[1][g], 0, w2q, xq[1], g)
+            product(banks[1][g], HALF, w1q, xq[1], g)
+            exp_z2(1, g)
+            exp_minus_z1(1, g)
+            make_odds(1, g)
+        make_square(1, 0, 2)
+        make_square(1, 2, G)
+        for g in range(G):
+            for h in range(2):
+                product(banks[0][g], h * HALF, w3q, xq[h], g)
+
+        moved = [tile("moved_%d" % h, [P, PACK, HALF], BF16) for h in range(2)]
+        for h in range(2):
+            for g in range(G):
+                share = tile("share_%d_%d" % (h, g), [P, HALF], F32)
+                nc.scalar.activation(
+                    out=share[:],
+                    in_=square[h][:, g * HALF : (g + 1) * HALF],
+                    func=ACT.Abs_reciprocal_sqrt,
+                    bias=1.0,
+                )
+                hh = tile("hh_%d_%d" % (h, g), [P, HALF], BF16)
+                nc.vector.scalar_tensor_tensor(
+                    out=hh[:],
+                    in0=banks[0][g][:, halves[h]],
+                    scalar=columns[:, ROWS * (G + g) : ROWS * (G + g) + 1],
+                    in1=share[:],
+                    op0=ALU.mult,
+                    op1=ALU.mult,
+                )
+                nc.sync.dma_start(out=moved[h][ROWS * g : ROWS * (g + 1), :, :], in_=hh[:])
+
+        wo_bf = tile("wo_bf", [P, O, PACK], BF16)
+        interleave_s(wo_bf, wo_raw, 0, O)
+        woq = quantize("wo", wo_bf, O)
+
+        y_banks = [banks[1], banks[0]]
+        for h in range(2):
+            hh_bf = tile("hh_bf_%d" % h, [P, HALF, PACK], BF16)
+            interleave_v(hh_bf, moved[h], 0, V_COLS)
+            interleave_s(hh_bf, moved[h], V_COLS, HALF)
+            hq = quantize("hh%d" % h, hh_bf, HALF)
+            for g in range(G):
+                product(y_banks[h][g], 0, woq, hq, g)
+        for h in range(2):
+            for g in range(G):
+                result = tile("result_%d_%d" % (h, g), [P, HALF], F32)
+                nc.vector.tensor_tensor(
+                    out=result[:], in0=y_banks[h][g][:, 0:HALF], in1=res_sb[:, g, halves[h]], op=ALU.add
+                )
+                nc.sync.dma_start(out=out[g, :, halves[h]], in_=result[:])

@@ -17,8 +17,10 @@ P = 128
 PACK = 4
 ROWS = 32
 HALF = N // 2
-MM_N = 128
-V_COLS = 160
+Q = 128
+X0_V_COLS = 64
+CHUNKS = ((0, 128), (128, 128), (256, 256))
+POOL_ADDS = ()
 
 
 def tile_rows_ftwoshare_kernel(tc, x, w1, w2, w3, re, hs, wo2, res, out):
@@ -31,26 +33,28 @@ def tile_rows_ftwoshare_kernel(tc, x, w1, w2, w3, re, hs, wo2, res, out):
         def tile(name, shape, dtype):
             return sb.tile(shape, dtype, name=name, align_bytes=64)
 
-        def load_packed(name, src, cols):
-            raw = tile(name, [P, PACK, cols.stop - cols.start], F32)
-            nc.sync.dma_start(out=raw[:], in_=src.rearrange("g (p j) c -> (g p) j c", j=PACK)[:, :, cols])
+        def load_packed(name, src, first):
+            raw = tile(name, [P, PACK, Q], F32)
+            nc.sync.dma_start(
+                out=raw[:], in_=src.rearrange("g (p j) c -> (g p) j c", j=PACK)[:, :, first : first + Q]
+            )
             return raw
 
-        def views(dst, raw, lo, hi):
-            return (
-                dst[:, lo:hi, :].rearrange("p (c i) j -> p c j i", i=4),
-                raw[:, :, lo:hi].rearrange("p j (c i) -> p c j i", i=4),
-            )
+        def views(dst, raw):
+            return dst.rearrange("p (c i) j -> p c j i", i=4), raw.rearrange("p j (c i) -> p c j i", i=4)
 
-        def interleave_v(dst, raw, lo, hi):
-            o, i = views(dst, raw, lo, hi)
+        def interleave_v(dst, raw):
+            o, i = views(dst, raw)
             nc.vector.tensor_copy(out=o, in_=i)
 
-        def interleave_s(dst, raw, lo, hi):
-            o, i = views(dst, raw, lo, hi)
+        def interleave_s(dst, raw):
+            o, i = views(dst, raw)
             nc.scalar.copy(out=o, in_=i)
 
-        def quantize(name, grouped, width):
+        def words(name, width=Q):
+            return tile(name, [P, width, PACK], BF16)
+
+        def quantize(name, grouped, width=Q):
             codes = tile(name + "_codes", [P, width], U32)
             scales = tile(name + "_scales", [P, width], U8)
             nc.vector.quantize_mx(
@@ -60,150 +64,203 @@ def tile_rows_ftwoshare_kernel(tc, x, w1, w2, w3, re, hs, wo2, res, out):
             )
             return codes, scales
 
-        def product(bank, at, weights, moving, g):
+        def product(bank, at, weights, moving, g, c=0):
             rows = slice(ROWS * g, ROWS * (g + 1))
-            for c in range(0, HALF, MM_N):
-                nc.tensor.matmul_mx(
-                    out=bank[:, at + c : at + c + MM_N],
-                    lhsT=weights[0][rows, :].bitcast(FP8X4),
-                    lhsT_scale=weights[1][rows, :],
-                    rhs=moving[0][rows, c : c + MM_N].bitcast(FP8X4),
-                    rhs_scale=moving[1][rows, c : c + MM_N],
-                    start=True,
-                    stop=True,
-                )
+            nc.tensor.matmul_mx(
+                out=bank[:, at : at + Q],
+                lhsT=weights[0][rows, :].bitcast(FP8X4),
+                lhsT_scale=weights[1][rows, :],
+                rhs=moving[0][rows, c : c + Q].bitcast(FP8X4),
+                rhs_scale=moving[1][rows, c : c + Q],
+                start=True,
+                stop=True,
+            )
 
         banks = [[ps.tile([P, N], F32, name="bank%d_%d" % (h, g)) for g in range(G)] for h in range(2)]
 
         rows_in = tile("rows_in", [P, 2 * G * ROWS], F32)
         nc.vector.memset(rows_in[:], 0.0)
+        w2_raw = load_packed("w2_raw", w2, 0)
+        x_raw = [load_packed("x0_raw", x, 0)]
+        w1_raw = load_packed("w1_raw", w1, 0)
+        x_raw.append(load_packed("x1_raw", x, Q))
         for k, src in enumerate((re, hs)):
-            nc.scalar.dma_start(
+            nc.sync.dma_start(
                 out=rows_in[0:P:ROWS, k * P : (k + 1) * P].rearrange("q (g b) -> q g b", g=G),
                 in_=src.rearrange("g (q b) o -> q g (b o)", b=ROWS),
             )
-
-        all_m = slice(0, M)
-        halves = [slice(0, HALF), slice(HALF, N)]
-        w2_raw = load_packed("w2_raw", w2, all_m)
-        xa_raw = load_packed("xa_raw", x, halves[0])
-        w1_raw = load_packed("w1_raw", w1, all_m)
-        xb_raw = load_packed("xb_raw", x, halves[1])
-        w3_raw = load_packed("w3_raw", w3, all_m)
-        wo_raw = load_packed("wo_raw", wo2, all_m)
+        x_raw.append(load_packed("x2_raw", x, 2 * Q))
+        x_raw.append(load_packed("x3_raw", x, 3 * Q))
+        w3_raw = load_packed("w3_raw", w3, 0)
+        wo_raw = load_packed("wo_raw", wo2, 0)
         res_sb = tile("res_sb", [P, G, N], F32)
         nc.sync.dma_start(out=res_sb[:], in_=res.rearrange("g o n -> o g n"))
 
-        w2_bf = tile("w2_bf", [P, M, PACK], BF16)
-        interleave_v(w2_bf, w2_raw, 0, M)
+        exps = [[tile("exps_%d_%d" % (h, g), [P, 2, 2, Q], F32) for g in range(G)] for h in range(2)]
+        odds = tile("odds", [P, G * N], F32)
+        square = tile("square", [P, G * N], F32)
+
+        def half_view(t, h):
+            width = min(w for n0, w in CHUNKS if n0 // HALF == h)
+            return t[:, h * G * HALF : (h + 1) * G * HALF].rearrange("p (c g n) -> p c g n", g=G, n=width)
         columns = tile("columns", [P, 2 * G * ROWS], F32)
-        nc.vector.transpose(out=columns[:], in_=rows_in[:])
-        w2q = quantize("w2", w2_bf, M)
 
-        xa_bf = tile("xa_bf", [P, HALF, PACK], BF16)
-        interleave_v(xa_bf, xa_raw, 0, V_COLS)
-        interleave_s(xa_bf, xa_raw, V_COLS, HALF)
-        xaq = quantize("xa", xa_bf, HALF)
-        w1_bf = tile("w1_bf", [P, M, PACK], BF16)
-        interleave_s(w1_bf, w1_raw, 0, M)
-        w1q = quantize("w1", w1_bf, M)
-        xb_bf = tile("xb_bf", [P, HALF, PACK], BF16)
-        interleave_v(xb_bf, xb_raw, 0, HALF)
-        xbq = quantize("xb", xb_bf, HALF)
-        xq = [xaq, xbq]
+        def odds_of_group(h, g):
+            if h == 0:
+                return half_view(odds, h)[:, :, g, :]
+            return half_view(odds, h)[:, 0, g, :].rearrange("p (c n) -> p c n", n=Q)
 
-        e2 = [[tile("e2_%d_%d" % (h, g), [P, HALF], F32) for g in range(G)] for h in range(2)]
-        inv_e1 = [[tile("inv_e1_%d_%d" % (h, g), [P, HALF], F32) for g in range(G)] for h in range(2)]
-        odds = [tile("odds_%d" % h, [P, G * HALF], F32) for h in range(2)]
-        square = [tile("square_%d" % h, [P, G * HALF], F32) for h in range(2)]
+        def scores(c):
+            for g in range(G):
+                bank = banks[(c + 1) % 2][g]
+                product(bank, 0, w2q, xq[c], g)
+                product(bank, Q, w1q, xq[c], g)
+                nc.scalar.activation(
+                    out=exps[c // 2][g][:, c % 2, :, :].rearrange("p z n -> p (z n)"),
+                    in_=bank[:, 0 : 2 * Q],
+                    func=ACT.Exp,
+                )
 
-        def exp_z2(h, g):
-            nc.scalar.activation(out=e2[h][g][:], in_=banks[h][g][:, 0:HALF], func=ACT.Exp)
-
-        def exp_minus_z1(h, g):
-            nc.scalar.activation(out=inv_e1[h][g][:], in_=banks[h][g][:, HALF:N], func=ACT.Exp, scale=-1.0)
-
-        def make_odds(h, g):
+        def make_odds(h, g, lo=0, hi=2):
             nc.vector.scalar_tensor_tensor(
-                out=odds[h][:, g * HALF : (g + 1) * HALF],
-                in0=e2[h][g][:],
+                out=odds_of_group(h, g),
+                in0=exps[h][g][:, lo:hi, 0, :],
                 scalar=columns[:, ROWS * g : ROWS * g + 1],
-                in1=inv_e1[h][g][:],
+                in1=exps[h][g][:, lo:hi, 1, :],
                 op0=ALU.add,
                 op1=ALU.mult,
             )
 
         def make_square(h, lo, hi):
-            cols = slice(lo * HALF, hi * HALF)
             nc.vector.scalar_tensor_tensor(
-                out=square[h][:, cols],
-                in0=odds[h][:, cols],
+                out=half_view(square, h)[:, :, lo:hi, :],
+                in0=half_view(odds, h)[:, :, lo:hi, :],
                 scalar=2.0,
-                in1=odds[h][:, cols],
+                in1=half_view(odds, h)[:, :, lo:hi, :],
                 op0=ALU.add,
                 op1=ALU.mult,
             )
 
+        w2_bf = words("w2_bf")
+        interleave_v(w2_bf[:], w2_raw[:])
+        x_bf = [words("x%d_bf" % c) for c in range(4)]
+        interleave_s(x_bf[0][:, X0_V_COLS:, :], x_raw[0][:, :, X0_V_COLS:])
+        w2q = quantize("w2", w2_bf)
+        interleave_v(x_bf[0][:, :X0_V_COLS, :], x_raw[0][:, :, :X0_V_COLS])
+        xq = [quantize("x0", x_bf[0])]
+        w1_bf = words("w1_bf")
+        w1_out, w1_in = views(w1_bf[:], w1_raw[:])
+        nc.scalar.activation(out=w1_out, in_=w1_in, func=ACT.Copy, scale=-1.0)
+        interleave_v(x_bf[1][:], x_raw[1][:])
+        w1q = quantize("w1", w1_bf)
+        for z, weights in enumerate((w2q, w1q)):
+            for g in range(G):
+                product(banks[z][g], 0, weights, xq[0], g)
+                nc.scalar.activation(out=exps[0][g][:, 0, z, :], in_=banks[z][g][:, 0:Q], func=ACT.Exp)
+        xq.append(quantize("x1", x_bf[1]))
+        scores(1)
+        interleave_v(x_bf[2][:], x_raw[2][:])
+        nc.vector.transpose(out=columns[:], in_=rows_in[:])
+        xq.append(quantize("x2", x_bf[2]))
+        scores(2)
+        interleave_v(x_bf[3][:], x_raw[3][:])
+        w3_bf = words("w3_bf")
+        interleave_v(w3_bf[:], w3_raw[:])
+        xq.append(quantize("x3", x_bf[3]))
+        scores(3)
+        w3q = quantize("w3", w3_bf)
         for g in range(G):
-            product(banks[0][g], 0, w2q, xq[0], g)
-            exp_z2(0, g)
-        for g in range(G):
-            product(banks[0][g], HALF, w1q, xq[0], g)
-            exp_minus_z1(0, g)
-            make_odds(0, g)
-        w3_bf = tile("w3_bf", [P, M, PACK], BF16)
-        interleave_v(w3_bf, w3_raw, 0, M)
-        make_square(0, 0, G)
-        w3q = quantize("w3", w3_bf, M)
-        for g in range(G):
-            product(banks[1][g], 0, w2q, xq[1], g)
-            product(banks[1][g], HALF, w1q, xq[1], g)
-            exp_z2(1, g)
-            exp_minus_z1(1, g)
-            make_odds(1, g)
-        make_square(1, 0, 2)
-        make_square(1, 2, G)
-        for g in range(G):
-            for h in range(2):
-                product(banks[0][g], h * HALF, w3q, xq[h], g)
-
-        moved = [tile("moved_%d" % h, [P, PACK, HALF], BF16) for h in range(2)]
+            for c in range(4):
+                product(banks[1][g], c * Q, w3q, xq[c], g)
         for h in range(2):
             for g in range(G):
-                share = tile("share_%d_%d" % (h, g), [P, HALF], F32)
+                make_odds(h, g)
+                if g == 2:
+                    make_square(h, 0, 2)
+            make_square(h, 2, G)
+
+        moved = {}
+        for n0, width in CHUNKS:
+            moved[n0] = tile("moved_%d" % n0, [P, PACK, width], BF16)
+            per_root = HALF // width
+            for g0 in range(0, G, per_root):
+                share = tile("share_%d_%d" % (n0, g0), [P, HALF], F32)
+                at = G * n0 + g0 * width
                 nc.scalar.activation(
-                    out=share[:],
-                    in_=square[h][:, g * HALF : (g + 1) * HALF],
-                    func=ACT.Abs_reciprocal_sqrt,
-                    bias=1.0,
+                    out=share[:], in_=square[:, at : at + HALF], func=ACT.Abs_reciprocal_sqrt, bias=1.0
                 )
-                hh = tile("hh_%d_%d" % (h, g), [P, HALF], BF16)
-                nc.vector.scalar_tensor_tensor(
-                    out=hh[:],
-                    in0=banks[0][g][:, halves[h]],
-                    scalar=columns[:, ROWS * (G + g) : ROWS * (G + g) + 1],
-                    in1=share[:],
-                    op0=ALU.mult,
-                    op1=ALU.mult,
-                )
-                nc.sync.dma_start(out=moved[h][ROWS * g : ROWS * (g + 1), :, :], in_=hh[:])
+                for g in range(g0, g0 + per_root):
+                    hh = tile("hh_%d_%d" % (n0, g), [P, width], BF16)
+                    nc.vector.scalar_tensor_tensor(
+                        out=hh[:],
+                        in0=banks[1][g][:, n0 : n0 + width],
+                        scalar=columns[:, ROWS * (G + g) : ROWS * (G + g) + 1],
+                        in1=share[:, (g - g0) * width : (g - g0 + 1) * width],
+                        op0=ALU.mult,
+                        op1=ALU.mult,
+                    )
+                    nc.sync.dma_start(out=moved[n0][ROWS * g : ROWS * (g + 1), :, :], in_=hh[:])
 
-        wo_bf = tile("wo_bf", [P, O, PACK], BF16)
-        interleave_s(wo_bf, wo_raw, 0, O)
-        woq = quantize("wo", wo_bf, O)
+        wo_bf = words("wo_bf")
+        interleave_s(wo_bf[:], wo_raw[:])
+        woq = quantize("wo", wo_bf)
 
-        y_banks = [banks[1], banks[0]]
-        for h in range(2):
-            hh_bf = tile("hh_bf_%d" % h, [P, HALF, PACK], BF16)
-            interleave_v(hh_bf, moved[h], 0, V_COLS)
-            interleave_s(hh_bf, moved[h], V_COLS, HALF)
-            hq = quantize("hh%d" % h, hh_bf, HALF)
-            for g in range(G):
-                product(y_banks[h][g], 0, woq, hq, g)
-        for h in range(2):
-            for g in range(G):
-                result = tile("result_%d_%d" % (h, g), [P, HALF], F32)
-                nc.vector.tensor_tensor(
-                    out=result[:], in0=y_banks[h][g][:, 0:HALF], in1=res_sb[:, g, halves[h]], op=ALU.add
-                )
-                nc.sync.dma_start(out=out[g, :, halves[h]], in_=result[:])
+        staged = {}
+
+        def regroup(n0, width, v_cols):
+            staged[n0] = words("hh_bf_%d" % n0, width)
+            first = max(c for c, w in CHUNKS if c <= n0)
+            src = moved[first][:, :, n0 - first : n0 - first + width]
+            if v_cols > 0:
+                interleave_v(staged[n0][:, :v_cols, :], src[:, :, :v_cols])
+            if v_cols < width:
+                interleave_s(staged[n0][:, v_cols:, :], src[:, :, v_cols:])
+
+        hq = {}
+
+        def second_quantize(n0, width):
+            hq[n0] = quantize("hh%d" % n0, staged[n0], width)
+
+        def second_product(n0, width, b, at, lo=0, hi=G):
+            for g in range(lo, hi):
+                for c in range(0, width, Q):
+                    product(banks[b][g], at + c, woq, hq[n0], g, c)
+
+        def finish(n0, width, b, at, g0, count):
+            result = tile("result_%d_%d" % (n0, g0), [P, count, width], F32)
+            for g in range(g0, g0 + count):
+                y = banks[b][g][:, at : at + width]
+                if (n0, g) in POOL_ADDS:
+                    y_sb = tile("y_%d_%d" % (n0, g), [P, width], F32)
+                    nc.scalar.copy(out=y_sb[:], in_=y)
+                    nc.gpsimd.tensor_tensor(
+                        out=result[:, g - g0, :], in0=y_sb[:], in1=res_sb[:, g, n0 : n0 + width], op=ALU.add
+                    )
+                else:
+                    nc.vector.tensor_tensor(
+                        out=result[:, g - g0, :], in0=y, in1=res_sb[:, g, n0 : n0 + width], op=ALU.add
+                    )
+            nc.sync.dma_start(
+                out=out[g0 : g0 + count, :, n0 : n0 + width].rearrange("g o n -> o g n"), in_=result[:]
+            )
+
+        regroup(0, 128, 80)
+        second_quantize(0, 128)
+        second_product(0, 128, 0, 0)
+        regroup(128, 128, 80)
+        second_quantize(128, 128)
+        second_product(128, 128, 1, 0)
+        finish(0, 128, 0, 0, 0, 4)
+        regroup(256, 128, 80)
+        regroup(384, 128, 0)
+        finish(128, 128, 1, 0, 0, 1)
+        second_quantize(256, 128)
+        second_product(256, 128, 0, 128)
+        finish(128, 128, 1, 0, 1, 3)
+        second_quantize(384, 128)
+        second_product(384, 128, 1, 128)
+        finish(256, 128, 0, 128, 0, 2)
+        finish(256, 128, 0, 128, 2, 2)
+        finish(384, 128, 1, 128, 0, 2)
+        finish(384, 128, 1, 128, 2, 1)
+        finish(384, 128, 1, 128, 3, 1)

from contextlib import ExitStack

import concourse.mybir as mybir

G, D, M, O, N = 4, 128, 128, 128, 512
FLOPS = 2 * G * N * (3 * D * M + M * O)

F32 = mybir.dt.float32
BF16 = mybir.dt.bfloat16
U32 = mybir.dt.uint32
U8 = mybir.dt.uint8
FP8X4 = mybir.dt.float8_e4m3fn_x4
ACT = mybir.ActivationFunctionType
ALU = mybir.AluOpType

P = 128
PACK = 4
ROWS = 32
HALF = N // 2
Q = 128
X0_V_COLS = 64
CHUNKS = ((0, 128), (128, 128), (256, 256))
POOL_ADDS = ()


def tile_rows_ftwoshare_kernel(tc, x, w1, w2, w3, re, hs, wo2, res, out):
    nc = tc.nc
    with ExitStack() as ctx:
        sb = ctx.enter_context(tc.tile_pool(name="sb", bufs=1))
        ps = ctx.enter_context(tc.psum_pool(name="ps", bufs=1))
        ctx.enter_context(tc.manual_schedule())

        def tile(name, shape, dtype):
            return sb.tile(shape, dtype, name=name, align_bytes=64)

        def load_packed(name, src, first):
            raw = tile(name, [P, PACK, Q], F32)
            nc.sync.dma_start(
                out=raw[:], in_=src.rearrange("g (p j) c -> (g p) j c", j=PACK)[:, :, first : first + Q]
            )
            return raw

        def views(dst, raw):
            return dst.rearrange("p (c i) j -> p c j i", i=4), raw.rearrange("p j (c i) -> p c j i", i=4)

        def interleave_v(dst, raw):
            o, i = views(dst, raw)
            nc.vector.tensor_copy(out=o, in_=i)

        def interleave_s(dst, raw):
            o, i = views(dst, raw)
            nc.scalar.copy(out=o, in_=i)

        def words(name, width=Q):
            return tile(name, [P, width, PACK], BF16)

        def quantize(name, grouped, width=Q):
            codes = tile(name + "_codes", [P, width], U32)
            scales = tile(name + "_scales", [P, width], U8)
            nc.vector.quantize_mx(
                out=codes[:].bitcast(FP8X4),
                scales=scales[:],
                in_=grouped[:].rearrange("p c j -> p (c j)"),
            )
            return codes, scales

        def product(bank, at, weights, moving, g, c=0):
            rows = slice(ROWS * g, ROWS * (g + 1))
            nc.tensor.matmul_mx(
                out=bank[:, at : at + Q],
                lhsT=weights[0][rows, :].bitcast(FP8X4),
                lhsT_scale=weights[1][rows, :],
                rhs=moving[0][rows, c : c + Q].bitcast(FP8X4),
                rhs_scale=moving[1][rows, c : c + Q],
                start=True,
                stop=True,
            )

        banks = [[ps.tile([P, N], F32, name="bank%d_%d" % (h, g)) for g in range(G)] for h in range(2)]

        rows_in = tile("rows_in", [P, 2 * G * ROWS], F32)
        nc.vector.memset(rows_in[:], 0.0)
        w2_raw = load_packed("w2_raw", w2, 0)
        x_raw = [load_packed("x0_raw", x, 0)]
        w1_raw = load_packed("w1_raw", w1, 0)
        x_raw.append(load_packed("x1_raw", x, Q))
        for k, src in enumerate((re, hs)):
            nc.sync.dma_start(
                out=rows_in[0:P:ROWS, k * P : (k + 1) * P].rearrange("q (g b) -> q g b", g=G),
                in_=src.rearrange("g (q b) o -> q g (b o)", b=ROWS),
            )
        x_raw.append(load_packed("x2_raw", x, 2 * Q))
        x_raw.append(load_packed("x3_raw", x, 3 * Q))
        w3_raw = load_packed("w3_raw", w3, 0)
        wo_raw = load_packed("wo_raw", wo2, 0)
        res_sb = tile("res_sb", [P, G, N], F32)
        nc.sync.dma_start(out=res_sb[:], in_=res.rearrange("g o n -> o g n"))

        exps = [[tile("exps_%d_%d" % (h, g), [P, 2, 2, Q], F32) for g in range(G)] for h in range(2)]
        odds = tile("odds", [P, G * N], F32)
        square = tile("square", [P, G * N], F32)

        def half_view(t, h):
            width = min(w for n0, w in CHUNKS if n0 // HALF == h)
            return t[:, h * G * HALF : (h + 1) * G * HALF].rearrange("p (c g n) -> p c g n", g=G, n=width)
        columns = tile("columns", [P, 2 * G * ROWS], F32)

        def odds_of_group(h, g):
            if h == 0:
                return half_view(odds, h)[:, :, g, :]
            return half_view(odds, h)[:, 0, g, :].rearrange("p (c n) -> p c n", n=Q)

        def scores(c):
            for g in range(G):
                bank = banks[(c + 1) % 2][g]
                product(bank, 0, w2q, xq[c], g)
                product(bank, Q, w1q, xq[c], g)
                nc.scalar.activation(
                    out=exps[c // 2][g][:, c % 2, :, :].rearrange("p z n -> p (z n)"),
                    in_=bank[:, 0 : 2 * Q],
                    func=ACT.Exp,
                )

        def make_odds(h, g, lo=0, hi=2):
            nc.vector.scalar_tensor_tensor(
                out=odds_of_group(h, g),
                in0=exps[h][g][:, lo:hi, 0, :],
                scalar=columns[:, ROWS * g : ROWS * g + 1],
                in1=exps[h][g][:, lo:hi, 1, :],
                op0=ALU.add,
                op1=ALU.mult,
            )

        def make_square(h, lo, hi):
            nc.vector.scalar_tensor_tensor(
                out=half_view(square, h)[:, :, lo:hi, :],
                in0=half_view(odds, h)[:, :, lo:hi, :],
                scalar=2.0,
                in1=half_view(odds, h)[:, :, lo:hi, :],
                op0=ALU.add,
                op1=ALU.mult,
            )

        w2_bf = words("w2_bf")
        interleave_v(w2_bf[:], w2_raw[:])
        x_bf = [words("x%d_bf" % c) for c in range(4)]
        interleave_s(x_bf[0][:, X0_V_COLS:, :], x_raw[0][:, :, X0_V_COLS:])
        w2q = quantize("w2", w2_bf)
        interleave_v(x_bf[0][:, :X0_V_COLS, :], x_raw[0][:, :, :X0_V_COLS])
        xq = [quantize("x0", x_bf[0])]
        w1_bf = words("w1_bf")
        w1_out, w1_in = views(w1_bf[:], w1_raw[:])
        nc.scalar.activation(out=w1_out, in_=w1_in, func=ACT.Copy, scale=-1.0)
        interleave_v(x_bf[1][:], x_raw[1][:])
        w1q = quantize("w1", w1_bf)
        for z, weights in enumerate((w2q, w1q)):
            for g in range(G):
                product(banks[z][g], 0, weights, xq[0], g)
                nc.scalar.activation(out=exps[0][g][:, 0, z, :], in_=banks[z][g][:, 0:Q], func=ACT.Exp)
        xq.append(quantize("x1", x_bf[1]))
        scores(1)
        interleave_v(x_bf[2][:], x_raw[2][:])
        nc.vector.transpose(out=columns[:], in_=rows_in[:])
        xq.append(quantize("x2", x_bf[2]))
        scores(2)
        interleave_v(x_bf[3][:], x_raw[3][:])
        w3_bf = words("w3_bf")
        interleave_v(w3_bf[:], w3_raw[:])
        xq.append(quantize("x3", x_bf[3]))
        scores(3)
        w3q = quantize("w3", w3_bf)
        for g in range(G):
            for c in range(4):
                product(banks[1][g], c * Q, w3q, xq[c], g)
        for h in range(2):
            for g in range(G):
                make_odds(h, g)
                if g == 2:
                    make_square(h, 0, 2)
            make_square(h, 2, G)

        moved = {}
        for n0, width in CHUNKS:
            moved[n0] = tile("moved_%d" % n0, [P, PACK, width], BF16)
            per_root = HALF // width
            for g0 in range(0, G, per_root):
                share = tile("share_%d_%d" % (n0, g0), [P, HALF], F32)
                at = G * n0 + g0 * width
                nc.scalar.activation(
                    out=share[:], in_=square[:, at : at + HALF], func=ACT.Abs_reciprocal_sqrt, bias=1.0
                )
                for g in range(g0, g0 + per_root):
                    hh = tile("hh_%d_%d" % (n0, g), [P, width], BF16)
                    nc.vector.scalar_tensor_tensor(
                        out=hh[:],
                        in0=banks[1][g][:, n0 : n0 + width],
                        scalar=columns[:, ROWS * (G + g) : ROWS * (G + g) + 1],
                        in1=share[:, (g - g0) * width : (g - g0 + 1) * width],
                        op0=ALU.mult,
                        op1=ALU.mult,
                    )
                    nc.sync.dma_start(out=moved[n0][ROWS * g : ROWS * (g + 1), :, :], in_=hh[:])

        wo_bf = words("wo_bf")
        interleave_s(wo_bf[:], wo_raw[:])
        woq = quantize("wo", wo_bf)

        staged = {}

        def regroup(n0, width, v_cols):
            staged[n0] = words("hh_bf_%d" % n0, width)
            first = max(c for c, w in CHUNKS if c <= n0)
            src = moved[first][:, :, n0 - first : n0 - first + width]
            if v_cols > 0:
                interleave_v(staged[n0][:, :v_cols, :], src[:, :, :v_cols])
            if v_cols < width:
                interleave_s(staged[n0][:, v_cols:, :], src[:, :, v_cols:])

        hq = {}

        def second_quantize(n0, width):
            hq[n0] = quantize("hh%d" % n0, staged[n0], width)

        def second_product(n0, width, b, at, lo=0, hi=G):
            for g in range(lo, hi):
                for c in range(0, width, Q):
                    product(banks[b][g], at + c, woq, hq[n0], g, c)

        def finish(n0, width, b, at, g0, count):
            result = tile("result_%d_%d" % (n0, g0), [P, count, width], F32)
            for g in range(g0, g0 + count):
                y = banks[b][g][:, at : at + width]
                if (n0, g) in POOL_ADDS:
                    y_sb = tile("y_%d_%d" % (n0, g), [P, width], F32)
                    nc.scalar.copy(out=y_sb[:], in_=y)
                    nc.gpsimd.tensor_tensor(
                        out=result[:, g - g0, :], in0=y_sb[:], in1=res_sb[:, g, n0 : n0 + width], op=ALU.add
                    )
                else:
                    nc.vector.tensor_tensor(
                        out=result[:, g - g0, :], in0=y, in1=res_sb[:, g, n0 : n0 + width], op=ALU.add
                    )
            nc.sync.dma_start(
                out=out[g0 : g0 + count, :, n0 : n0 + width].rearrange("g o n -> o g n"), in_=result[:]
            )

        regroup(0, 128, 80)
        second_quantize(0, 128)
        second_product(0, 128, 0, 0)
        regroup(128, 128, 80)
        second_quantize(128, 128)
        second_product(128, 128, 1, 0)
        finish(0, 128, 0, 0, 0, 4)
        regroup(256, 128, 80)
        regroup(384, 128, 0)
        finish(128, 128, 1, 0, 0, 1)
        second_quantize(256, 128)
        second_product(256, 128, 0, 128)
        finish(128, 128, 1, 0, 1, 3)
        second_quantize(384, 128)
        second_product(384, 128, 1, 128)
        finish(256, 128, 0, 128, 0, 2)
        finish(256, 128, 0, 128, 2, 2)
        finish(384, 128, 1, 128, 0, 2)
        finish(384, 128, 1, 128, 2, 1)
        finish(384, 128, 1, 128, 3, 1)
